import numpy as np
import ml_dtypes


def mxq(x, axis, fmt="e4m3"):
    dtype, down = {"e4m3": (ml_dtypes.float8_e4m3fn, 7), "e5m2": (ml_dtypes.float8_e5m2, 14)}[fmt]
    v = np.moveaxis(np.asarray(x, np.float32).astype(ml_dtypes.bfloat16).astype(np.float64), axis, -1)
    blocks = v.reshape(v.shape[:-1] + (-1, 32))
    amax = np.abs(blocks).max(-1, keepdims=True)
    byte = np.maximum(np.where(amax > 0, np.frexp(amax)[1] - 1 + 127, 0) - down, 1)
    scale = np.exp2(byte - 127.0)
    codes = (blocks / scale).astype(np.float32).astype(dtype).astype(np.float64)
    return np.moveaxis((codes * scale).reshape(v.shape), -1, axis)


WIDE = False


def mx_kscale(k):
    if not WIDE:
        return np.ones(k)
    levels = np.array([10, -10, 5, -5, 0])
    if k % 512:
        return np.exp2(np.random.permutation(np.resize(levels, k // 32))).repeat(32)
    a = np.empty((k // 512, 16))
    for p in range(k // 512):
        a[p, :8] = np.random.permutation(np.resize(levels, 8))
        for g in range(8):
            far = levels[np.abs(levels - a[p, g]) >= 10]
            a[p, g + 8] = far[np.random.randint(len(far))]
    return np.exp2(a.ravel()).repeat(32)


def f64(x):
    return np.asarray(x).astype(np.float64)


def striped(idx):
    return np.tile(idx.reshape(-1, 16).T, (8, 1)).astype(np.uint16)


def unstriped(offs):
    return offs[:16].T.reshape(-1).astype(np.int64)


E2M1 = np.array([0.0, 0.5, 1.0, 1.5, 2.0, 3.0, 4.0, 6.0, -0.0, -0.5, -1.0, -1.5, -2.0, -3.0, -4.0, -6.0])


def pack_weight(w, fmt):
    k, n = w.shape
    w = f64(np.asarray(w, np.float32).astype(ml_dtypes.bfloat16)).reshape(k // 32, 32, n)
    amax = np.abs(w).max(1)
    if fmt == "e4m3":
        byte = np.frexp(amax)[1] - 1 + 127 - 7
    else:
        mant, ex = np.frexp(amax / 6.0)
        byte = np.where(mant > 0.5, ex, ex - 1) + 127
    byte = np.clip(np.where(amax > 0, byte, 1), 1, 254)
    scaled = (w * np.exp2(127.0 - byte)[:, None, :]).reshape(k, n).astype(np.float32)
    by_word = np.ascontiguousarray(scaled.reshape(k // 512, 128, 4, n).transpose(0, 1, 3, 2))
    if fmt == "e4m3":
        words = by_word.astype(ml_dtypes.float8_e4m3fn).view(np.uint8)
    else:
        c = by_word.astype(ml_dtypes.float4_e2m1fn).view(np.uint8) & 0xF
        words = (c[..., 0::2] | (c[..., 1::2] << 4)).reshape(k // 512, 128, 2 * n)
    return np.ascontiguousarray(words), np.ascontiguousarray(byte.astype(np.uint8).reshape(k // 512, 16, n))


def unpack_weight(words, scales, fmt):
    g, _, n = scales.shape
    words = np.ascontiguousarray(words).reshape(g, 128, n, -1)
    if fmt == "e4m3":
        vals = words.view(ml_dtypes.float8_e4m3fn).astype(np.float64)
    else:
        nib = np.empty((g, 128, n, 4), np.uint8)
        nib[..., 0::2] = words & 0xF
        nib[..., 1::2] = words >> 4
        vals = E2M1[nib]
    vals = vals * np.repeat(np.exp2(scales.astype(np.float64) - 127.0), 8, axis=1)[..., None]
    return vals.transpose(0, 1, 3, 2).reshape(g * 512, n)


def gelu(v):
    return 0.5 * v * (1.0 + np.tanh(np.sqrt(2.0 / np.pi) * (v + 0.044715 * v**3)))


K, T, E, C, N = 512, 4096, 16, 128, 128


def by_expert(wq, xq):
    return np.concatenate([wq[e].T @ xq[:, e * C:(e + 1) * C] for e in range(E)], axis=1)


def setup_inputs():
    n = np.random.standard_normal
    s = mx_kscale(K)[:, None]
    w = [pack_weight(m, "e2m1") for m in n((E, K, N)) / np.sqrt(K) / s[None]]
    return {
        "xT": (n((K, T)) * s).astype(np.float32),
        "w_words": np.stack([m[0] for m in w]),
        "w_scales": np.stack([m[1] for m in w]),
        "b": (0.3 * n((N, E))).astype(np.float32),
        "gate": np.tile(np.random.uniform(0.2, 1.0, E * C), (N, 1)).astype(np.float32),
        "offs": striped(np.random.permutation(T)[:E * C]),
        "dst": striped(np.random.permutation(T)[:E * C]),
    }


def reference(xT, w_words, w_scales, b, gate, offs, dst):
    idx = unstriped(offs)
    w = np.stack([unpack_weight(w_words[e], w_scales[e], "e2m1") for e in range(E)])
    xq = mxq(f64(xT)[:, idx], 0, "e4m3")
    y = by_expert(w, xq)
    y = gelu(y + np.repeat(f64(b), C, axis=1))
    out = np.zeros((N, T))
    out[:, unstriped(dst)] = f64(gate) * y
    return out

@@ -1,0 +1,126 @@
+import concourse.mybir as mybir
+
+T, E, SLOTS, N = 4096, 16, 2048, 128
+FLOPS = 2 * SLOTS * 512 * N
+
+F32 = mybir.dt.float32
+BF16 = mybir.dt.bfloat16
+I32 = mybir.dt.int32
+U32 = mybir.dt.uint32
+U16 = mybir.dt.uint16
+U8 = mybir.dt.uint8
+FP8X4 = mybir.dt.float8_e4m3fn_x4
+FP4X4 = mybir.dt.float4_e2m1fn_x4
+
+P = 128
+GROUPS = 4
+GS = SLOTS // GROUPS
+EG = E // GROUPS
+
+
+def tile_moe_two_lin_gelu_kernel(tc, xT, w_words, w_scales, b, gate, offs, dst, out):
+    nc = tc.nc
+    gelu = mybir.ActivationFunctionType.Gelu_apprx_tanh
+    mult = mybir.AluOpType.mult
+
+    with tc.tile_pool(name="keep", bufs=1) as keep, tc.psum_pool(name="psum", bufs=1) as psum:
+        offs_t = keep.tile([P, SLOTS // 16], U16, name="offs_t")
+        dst_t = keep.tile([P, SLOTS // 16], U16, name="dst_t")
+        x = [keep.tile([P, T], F32, name=f"x{t}") for t in range(4)]
+        pairs = [keep.tile([P, 2, SLOTS], F32, name=f"pairs{u}") for u in range(2)]
+        grouped = [keep.tile([P, GS, 4], BF16, name=f"grouped{g}", align_bytes=64) for g in range(GROUPS)]
+        codes = [keep.tile([P, GS], U32, name=f"codes{g}", align_bytes=64) for g in range(GROUPS)]
+        scales = [keep.tile([P, GS], U8, name=f"scales{g}", align_bytes=64) for g in range(GROUPS)]
+        w_t = keep.tile([P, E, 2 * N], U8, name="w_t", align_bytes=64)
+        ws_t = keep.tile([P, E, N], U8, name="ws_t", align_bytes=64)
+        b_t = keep.tile([P, E], F32, name="b_t")
+        gate_t = [keep.tile([P, GS], F32, name=f"gate{g}") for g in range(GROUPS)]
+        y = [keep.tile([P, GS], F32, name=f"y{g}") for g in range(GROUPS)]
+        out_t = keep.tile([P, T], F32, name="out_t")
+        warm = keep.tile([P, 1], F32, name="warm")
+        acc = [psum.tile([P, GS], F32, name=f"acc{g}") for g in range(GROUPS)]
+
+        nc.sync.dma_start(offs_t[:], offs)
+        x_planes = xT.rearrange("(p t) w -> p t w", t=4)
+        for t in range(4):
+            nc.sync.dma_start(out=x[t][:], in_=x_planes[:, t, :])
+
+        nc.vector.memset(warm[:], 0.0)
+        nc.scalar.activation(out=warm[:], in_=warm[:], func=gelu)
+        nc.vector.memset(ws_t[:].rearrange("p e n -> p (e n)").bitcast(I32), 0)
+        nc.gpsimd.memset(out_t[:], 0.0)
+
+        nc.sync.dma_start(b_t[:], b)
+        ws_rows = w_scales.bitcast(I32).rearrange("e a q n -> (a q) e n")
+        for q in range(4):
+            nc.sync.dma_start(out=ws_t[32 * q : 32 * q + 4, :, :].bitcast(I32), in_=ws_rows[4 * q : 4 * q + 4])
+        w_rows = w_words.bitcast(I32).rearrange("e a p n -> p (e a) n")
+        nc.sync.dma_start(out=w_t[:, 0:EG, :].bitcast(I32), in_=w_rows[:, 0:EG, :])
+        nc.sync.dma_start(dst_t[:], dst)
+        nc.sync.dma_start(out=gate_t[0][:], in_=gate[:, 0:GS])
+        nc.sync.dma_start(out=w_t[:, EG:E, :].bitcast(I32), in_=w_rows[:, EG:E, :])
+        for g in range(1, GROUPS):
+            nc.sync.dma_start(out=gate_t[g][:], in_=gate[:, g * GS : (g + 1) * GS])
+
+        def cols(g):
+            return slice(g * GS, (g + 1) * GS)
+
+        def lists(tile, g):
+            return tile[:, g * (GS // 16) : (g + 1) * (GS // 16)]
+
+        def gather(t, g):
+            nc.vector.tensor_copy(pairs[t // 2][:, t % 2, cols(g)], x[t][:].indirect(lists(offs_t, g)))
+
+        def interleave(u, g):
+            nc.scalar.copy(out=grouped[g][:, :, 2 * u : 2 * u + 2], in_=pairs[u][:, :, cols(g)].rearrange("p u n -> p n u"))
+
+        def quantize(g):
+            nc.vector.quantize_mx(out=codes[g][:].bitcast(FP8X4), scales=scales[g][:], in_=grouped[g][:].rearrange("p n t -> p (n t)"))
+
+        def multiply(g):
+            for i in range(EG):
+                e = g * EG + i
+                c = slice(i * N, (i + 1) * N)
+                nc.tensor.matmul_mx(
+                    out=acc[g][:, c],
+                    lhsT=w_t[:, e, :].bitcast(FP4X4),
+                    lhsT_scale=ws_t[:, e, :],
+                    rhs=codes[g][:, c].bitcast(FP8X4),
+                    rhs_scale=scales[g][:, c],
+                    start=True,
+                    stop=True,
+                )
+            for i in range(EG):
+                e = g * EG + i
+                c = slice(i * N, (i + 1) * N)
+                nc.scalar.activation(out=y[g][:, c], in_=acc[g][:, c], func=gelu, bias=b_t[:, e : e + 1])
+
+        def scatter(g):
+            nc.vector.tensor_tensor(out_t[:].indirect(lists(dst_t, g)), y[g][:], gate_t[g][:], mult)
+
+        nc.vector.tensor_copy(pairs[0][:, 0, :], x[0][:].indirect(offs_t[:]))
+        for g in range(GROUPS):
+            gather(1, g)
+            interleave(0, g)
+        nc.vector.tensor_copy(pairs[1][:, 0, :], x[2][:].indirect(offs_t[:]))
+        gather(3, 0)
+        interleave(1, 0)
+        gather(3, 1)
+        quantize(0)
+        multiply(0)
+        interleave(1, 1)
+        gather(3, 2)
+        gather(3, 3)
+        quantize(1)
+        multiply(1)
+        interleave(1, 2)
+        interleave(1, 3)
+        scatter(0)
+        quantize(2)
+        multiply(2)
+        scatter(1)
+        quantize(3)
+        multiply(3)
+        scatter(2)
+        scatter(3)
+        nc.sync.dma_start(out, out_t[:])

@@ -13,9 +13,13 @@ FP8X4 = mybir.dt.float8_e4m3fn_x4
 FP4X4 = mybir.dt.float4_e2m1fn_x4
 
 P = 128
-GROUPS = 4
-GS = SLOTS // GROUPS
-EG = E // GROUPS
+G = 512
+A, B, C, D = range(4)
+CHUNKS = (((0, 2048), (2048, 3072), (3072, 4096)), ((0, 1536), (1536, 3072), (3072, 3584), (3584, 4096)))
+CASTS = (
+    (("v", 0, 1280), ("s", 1280, 2048), ("v", 2048, 3072), ("v", 3072, 3712), ("s", 3712, 4096)),
+    (("s", 0, 1536), ("s", 1536, 2048), ("v", 2048, 3072), ("s", 3072, 3584), ("v", 3584, 3840), ("s", 3840, 4096)),
+)
 
 
 def tile_moe_two_lin_gelu_kernel(tc, xT, w_words, w_scales, b, gate, offs, dst, out):
@@ -26,101 +30,116 @@ def tile_moe_two_lin_gelu_kernel(tc, xT, w_words, w_scales, b, gate, offs, dst, 
     with tc.tile_pool(name="keep", bufs=1) as keep, tc.psum_pool(name="psum", bufs=1) as psum:
         offs_t = keep.tile([P, SLOTS // 16], U16, name="offs_t")
         dst_t = keep.tile([P, SLOTS // 16], U16, name="dst_t")
-        x = [keep.tile([P, T], F32, name=f"x{t}") for t in range(4)]
-        pairs = [keep.tile([P, 2, SLOTS], F32, name=f"pairs{u}") for u in range(2)]
-        grouped = [keep.tile([P, GS, 4], BF16, name=f"grouped{g}", align_bytes=64) for g in range(GROUPS)]
-        codes = [keep.tile([P, GS], U32, name=f"codes{g}", align_bytes=64) for g in range(GROUPS)]
-        scales = [keep.tile([P, GS], U8, name=f"scales{g}", align_bytes=64) for g in range(GROUPS)]
+        raw = [[keep.tile([P, 2, c1 - c0], F32, name=f"raw{u}_{c0}") for c0, c1 in CHUNKS[u]] for u in range(2)]
+        words = [keep.tile([P, 2 * T], BF16, name=f"words{u}", align_bytes=64) for u in range(2)]
+        grouped_ab = keep.tile([P, 8 * G], BF16, name="grouped_ab", align_bytes=64)
+        grouped_cd = keep.tile([P, 8 * G], BF16, name="grouped_cd", align_bytes=64)
+        codes = keep.tile([P, SLOTS], U32, name="codes", align_bytes=64)
+        late_cd = keep.tile([P, 4 * G], BF16, name="late_cd", align_bytes=64)
+        scales = keep.tile([P, SLOTS], U8, name="scales", align_bytes=64)
         w_t = keep.tile([P, E, 2 * N], U8, name="w_t", align_bytes=64)
         ws_t = keep.tile([P, E, N], U8, name="ws_t", align_bytes=64)
         b_t = keep.tile([P, E], F32, name="b_t")
-        gate_t = [keep.tile([P, GS], F32, name=f"gate{g}") for g in range(GROUPS)]
-        y = [keep.tile([P, GS], F32, name=f"y{g}") for g in range(GROUPS)]
+        gate_t = [keep.tile([P, n], F32, name=f"gate{i}") for i, n in enumerate((G, 3 * G))]
+        y_a = keep.tile([P, G], F32, name="y_a")
+        y_bcd = keep.tile([P, 3 * G], F32, name="y_bcd")
         out_t = keep.tile([P, T], F32, name="out_t")
         warm = keep.tile([P, 1], F32, name="warm")
-        acc = [psum.tile([P, GS], F32, name=f"acc{g}") for g in range(GROUPS)]
+        acc = [psum.tile([P, G], F32, name=f"acc{g}") for g in range(4)]
 
-        nc.sync.dma_start(offs_t[:], offs)
-        x_planes = xT.rearrange("(p t) w -> p t w", t=4)
-        for t in range(4):
-            nc.sync.dma_start(out=x[t][:], in_=x_planes[:, t, :])
+        x_rows = xT.rearrange("(p t) w -> p t w", t=4)
+        ws_rows = w_scales.bitcast(I32).rearrange("e a q n -> (a q) e n")
+        w_rows = w_words.bitcast(I32).rearrange("e a p n -> p (e a) n")
+
+        def load_weights(e0, e1):
+            for q in range(4):
+                nc.sync.dma_start(out=ws_t[32 * q : 32 * q + 4, e0:e1, :].bitcast(I32), in_=ws_rows[4 * q : 4 * q + 4, e0:e1])
+            nc.sync.dma_start(out=w_t[:, e0:e1, :].bitcast(I32), in_=w_rows[:, e0:e1, :])
+
+        def load_chunk(u, i):
+            c0, c1 = CHUNKS[u][i]
+            nc.sync.dma_start(out=raw[u][i][:], in_=x_rows[:, 2 * u : 2 * u + 2, c0:c1])
 
         nc.vector.memset(warm[:], 0.0)
         nc.scalar.activation(out=warm[:], in_=warm[:], func=gelu)
         nc.vector.memset(ws_t[:].rearrange("p e n -> p (e n)").bitcast(I32), 0)
         nc.gpsimd.memset(out_t[:], 0.0)
 
+        load_chunk(0, 0)
+        nc.sync.dma_start(offs_t[:], offs)
+        for u in range(2):
+            for i in range(1 - u, len(CHUNKS[u])):
+                load_chunk(u, i)
+        load_weights(0, 4)
         nc.sync.dma_start(b_t[:], b)
-        ws_rows = w_scales.bitcast(I32).rearrange("e a q n -> (a q) e n")
-        for q in range(4):
-            nc.sync.dma_start(out=ws_t[32 * q : 32 * q + 4, :, :].bitcast(I32), in_=ws_rows[4 * q : 4 * q + 4])
-        w_rows = w_words.bitcast(I32).rearrange("e a p n -> p (e a) n")
-        nc.sync.dma_start(out=w_t[:, 0:EG, :].bitcast(I32), in_=w_rows[:, 0:EG, :])
+        load_weights(4, E)
         nc.sync.dma_start(dst_t[:], dst)
-        nc.sync.dma_start(out=gate_t[0][:], in_=gate[:, 0:GS])
-        nc.sync.dma_start(out=w_t[:, EG:E, :].bitcast(I32), in_=w_rows[:, EG:E, :])
-        for g in range(1, GROUPS):
-            nc.sync.dma_start(out=gate_t[g][:], in_=gate[:, g * GS : (g + 1) * GS])
+        for i, (s0, s1) in enumerate(((0, G), (G, 4 * G))):
+            nc.sync.dma_start(out=gate_t[i][:], in_=gate[:, s0:s1])
 
-        def cols(g):
-            return slice(g * GS, (g + 1) * GS)
+        def slots(grouped, s0, s1):
+            return grouped[:, 4 * s0 : 4 * s1].rearrange("p (n t) -> p n t", t=4)
 
-        def lists(tile, g):
-            return tile[:, g * (GS // 16) : (g + 1) * (GS // 16)]
+        def cast(u, engine, c0, c1):
+            i = [c[0] <= c0 and c1 <= c[1] for c in CHUNKS[u]].index(True)
+            base = CHUNKS[u][i][0]
+            to = words[u][:, 2 * c0 : 2 * c1].rearrange("p (n t) -> p n t", t=2)
+            src = raw[u][i][:, :, c0 - base : c1 - base].rearrange("p t n -> p n t")
+            if engine == "v":
+                nc.vector.tensor_copy(out=to, in_=src)
+            else:
+                nc.scalar.copy(out=to, in_=src)
 
-        def gather(t, g):
-            nc.vector.tensor_copy(pairs[t // 2][:, t % 2, cols(g)], x[t][:].indirect(lists(offs_t, g)))
+        def gather(to, u, s0, s1):
+            nc.vector.tensor_copy(to, words[u][:].bitcast(U32).indirect(offs_t[:, s0 // 16 : s1 // 16]))
 
-        def interleave(u, g):
-            nc.scalar.copy(out=grouped[g][:, :, 2 * u : 2 * u + 2], in_=pairs[u][:, :, cols(g)].rearrange("p u n -> p n u"))
+        def stepped(grouped, u):
+            return grouped[:].bitcast(U32).rearrange("p (n u) -> p u n", u=2)[:, u, :]
 
-        def quantize(g):
-            nc.vector.quantize_mx(out=codes[g][:].bitcast(FP8X4), scales=scales[g][:], in_=grouped[g][:].rearrange("p n t -> p (n t)"))
+        def merge(grouped, late, s0, s1):
+            nc.scalar.copy(out=slots(grouped, s0, s1)[:, :, 2:4], in_=late[:, 2 * s0 : 2 * s1].rearrange("p (n t) -> p n t", t=2))
 
-        def multiply(g):
-            for i in range(EG):
-                e = g * EG + i
-                c = slice(i * N, (i + 1) * N)
-                nc.tensor.matmul_mx(
-                    out=acc[g][:, c],
-                    lhsT=w_t[:, e, :].bitcast(FP4X4),
-                    lhsT_scale=ws_t[:, e, :],
-                    rhs=codes[g][:, c].bitcast(FP8X4),
-                    rhs_scale=scales[g][:, c],
-                    start=True,
-                    stop=True,
-                )
-            for i in range(EG):
-                e = g * EG + i
-                c = slice(i * N, (i + 1) * N)
-                nc.scalar.activation(out=y[g][:, c], in_=acc[g][:, c], func=gelu, bias=b_t[:, e : e + 1])
+        def quantize(grouped, s0, s1):
+            nc.vector.quantize_mx(out=codes[:, s0:s1].bitcast(FP8X4), scales=scales[:, s0:s1], in_=grouped)
 
-        def scatter(g):
-            nc.vector.tensor_tensor(out_t[:].indirect(lists(dst_t, g)), y[g][:], gate_t[g][:], mult)
+        def multiply(g, y, y_base):
+            for pass_kind in ("matmul", "gelu"):
+                for i in range(4):
+                    e = 4 * g + i
+                    a = acc[g][:, i * N : (i + 1) * N]
+                    if pass_kind == "matmul":
+                        nc.tensor.matmul_mx(
+                            out=a,
+                            lhsT=w_t[:, e, :].bitcast(FP4X4),
+                            lhsT_scale=ws_t[:, e, :],
+                            rhs=codes[:, e * N : (e + 1) * N].bitcast(FP8X4),
+                            rhs_scale=scales[:, e * N : (e + 1) * N],
+                            start=True,
+                            stop=True,
+                        )
+                    else:
+                        nc.scalar.activation(out=y[:, e * N - y_base : (e + 1) * N - y_base], in_=a, func=gelu, bias=b_t[:, e : e + 1])
 
-        nc.vector.tensor_copy(pairs[0][:, 0, :], x[0][:].indirect(offs_t[:]))
-        for g in range(GROUPS):
-            gather(1, g)
-            interleave(0, g)
-        nc.vector.tensor_copy(pairs[1][:, 0, :], x[2][:].indirect(offs_t[:]))
-        gather(3, 0)
-        interleave(1, 0)
-        gather(3, 1)
-        quantize(0)
-        multiply(0)
-        interleave(1, 1)
-        gather(3, 2)
-        gather(3, 3)
-        quantize(1)
-        multiply(1)
-        interleave(1, 2)
-        interleave(1, 3)
-        scatter(0)
-        quantize(2)
-        multiply(2)
-        scatter(1)
-        quantize(3)
-        multiply(3)
-        scatter(2)
-        scatter(3)
+        def scatter(i, y, s0, s1):
+            nc.vector.tensor_tensor(out_t[:].indirect(dst_t[:, s0 // 16 : s1 // 16]), y[:], gate_t[i][:], mult)
+
+        for c in CASTS[0]:
+            cast(0, *c)
+        gather(stepped(grouped_ab, 0), 0, 0, 2 * G)
+        gather(stepped(grouped_cd, 0), 0, 2 * G, 4 * G)
+        for c in CASTS[1]:
+            cast(1, *c)
+        gather(late_cd[:].bitcast(U32), 1, 2 * G, 4 * G)
+        merge(grouped_cd, late_cd, 0, G)
+        merge(grouped_cd, late_cd, G, 2 * G)
+        gather(stepped(grouped_ab, 1), 1, 0, 2 * G)
+        quantize(grouped_ab[:, 0 : 4 * G], 0, G)
+        multiply(A, y_a, 0)
+        quantize(grouped_ab[:, 4 * G : 8 * G], G, 2 * G)
+        multiply(B, y_bcd, G)
+        quantize(grouped_cd[:], 2 * G, 4 * G)
+        multiply(C, y_bcd, G)
+        multiply(D, y_bcd, G)
+        scatter(0, y_a, 0, G)
+        scatter(1, y_bcd, G, 4 * G)
         nc.sync.dma_start(out, out_t[:])

@@ -30,7 +30,8 @@ def tile_moe_two_lin_gelu_kernel(tc, xT, w_words, w_scales, b, gate, offs, dst, 
     with tc.tile_pool(name="keep", bufs=1) as keep, tc.psum_pool(name="psum", bufs=1) as psum:
         offs_t = keep.tile([P, SLOTS // 16], U16, name="offs_t")
         dst_t = keep.tile([P, SLOTS // 16], U16, name="dst_t")
-        raw = [[keep.tile([P, 2, c1 - c0], F32, name=f"raw{u}_{c0}") for c0, c1 in CHUNKS[u]] for u in range(2)]
+        raw_0 = keep.tile([P, 2, T], F32, name="raw_0")
+        raw_1 = [keep.tile([P, 2, c1 - c0], F32, name=f"raw_1_{c0}") for c0, c1 in CHUNKS[1]]
         words = [keep.tile([P, 2 * T], BF16, name=f"words{u}", align_bytes=64) for u in range(2)]
         grouped_ab = keep.tile([P, 8 * G], BF16, name="grouped_ab", align_bytes=64)
         grouped_cd = keep.tile([P, 8 * G], BF16, name="grouped_cd", align_bytes=64)
@@ -56,20 +57,17 @@ def tile_moe_two_lin_gelu_kernel(tc, xT, w_words, w_scales, b, gate, offs, dst, 
                 nc.sync.dma_start(out=ws_t[32 * q : 32 * q + 4, e0:e1, :].bitcast(I32), in_=ws_rows[4 * q : 4 * q + 4, e0:e1])
             nc.sync.dma_start(out=w_t[:, e0:e1, :].bitcast(I32), in_=w_rows[:, e0:e1, :])
 
-        def load_chunk(u, i):
-            c0, c1 = CHUNKS[u][i]
-            nc.sync.dma_start(out=raw[u][i][:], in_=x_rows[:, 2 * u : 2 * u + 2, c0:c1])
-
         nc.vector.memset(warm[:], 0.0)
         nc.scalar.activation(out=warm[:], in_=warm[:], func=gelu)
         nc.vector.memset(ws_t[:].rearrange("p e n -> p (e n)").bitcast(I32), 0)
         nc.gpsimd.memset(out_t[:], 0.0)
 
-        load_chunk(0, 0)
+        nc.sync.dma_start(out=raw_0[:, 0, :], in_=x_rows[:, 0, :])
         nc.sync.dma_start(offs_t[:], offs)
-        for u in range(2):
-            for i in range(1 - u, len(CHUNKS[u])):
-                load_chunk(u, i)
+        for c0, c1 in CHUNKS[0]:
+            nc.sync.dma_start(out=raw_0[:, 1, c0:c1], in_=x_rows[:, 1, c0:c1])
+        for i, (c0, c1) in enumerate(CHUNKS[1]):
+            nc.sync.dma_start(out=raw_1[i][:], in_=x_rows[:, 2:4, c0:c1])
         load_weights(0, 4)
         nc.sync.dma_start(b_t[:], b)
         load_weights(4, E)
@@ -81,10 +79,14 @@ def tile_moe_two_lin_gelu_kernel(tc, xT, w_words, w_scales, b, gate, offs, dst, 
             return grouped[:, 4 * s0 : 4 * s1].rearrange("p (n t) -> p n t", t=4)
 
         def cast(u, engine, c0, c1):
-            i = [c[0] <= c0 and c1 <= c[1] for c in CHUNKS[u]].index(True)
-            base = CHUNKS[u][i][0]
+            if u == 0:
+                raw = raw_0[:, :, c0:c1]
+            else:
+                i = [c[0] <= c0 and c1 <= c[1] for c in CHUNKS[1]].index(True)
+                base = CHUNKS[1][i][0]
+                raw = raw_1[i][:, :, c0 - base : c1 - base]
             to = words[u][:, 2 * c0 : 2 * c1].rearrange("p (n t) -> p n t", t=2)
-            src = raw[u][i][:, :, c0 - base : c1 - base].rearrange("p t n -> p n t")
+            src = raw.rearrange("p t n -> p n t")
             if engine == "v":
                 nc.vector.tensor_copy(out=to, in_=src)
             else:
@@ -132,7 +134,8 @@ def tile_moe_two_lin_gelu_kernel(tc, xT, w_words, w_scales, b, gate, offs, dst, 
         gather(late_cd[:].bitcast(U32), 1, 2 * G, 4 * G)
         merge(grouped_cd, late_cd, 0, G)
         merge(grouped_cd, late_cd, G, 2 * G)
-        gather(stepped(grouped_ab, 1), 1, 0, 2 * G)
+        gather(stepped(grouped_ab, 1)[:, 0:G], 1, 0, G)
+        gather(stepped(grouped_ab, 1)[:, G : 2 * G], 1, G, 2 * G)
         quantize(grouped_ab[:, 0 : 4 * G], 0, G)
         multiply(A, y_a, 0)
         quantize(grouped_ab[:, 4 * G : 8 * G], G, 2 * G)

import concourse.mybir as mybir

T, E, SLOTS, N = 4096, 16, 2048, 128
FLOPS = 2 * SLOTS * 512 * N

F32 = mybir.dt.float32
BF16 = mybir.dt.bfloat16
I32 = mybir.dt.int32
U32 = mybir.dt.uint32
U16 = mybir.dt.uint16
U8 = mybir.dt.uint8
FP8X4 = mybir.dt.float8_e4m3fn_x4
FP4X4 = mybir.dt.float4_e2m1fn_x4

P = 128
G = 512
A, B, C, D = range(4)
CHUNKS = (((0, 2048), (2048, 3072), (3072, 4096)), ((0, 1536), (1536, 3072), (3072, 3584), (3584, 4096)))
CASTS = (
    (("v", 0, 1280), ("s", 1280, 2048), ("v", 2048, 3072), ("v", 3072, 3712), ("s", 3712, 4096)),
    (("s", 0, 1536), ("s", 1536, 2048), ("v", 2048, 3072), ("s", 3072, 3584), ("v", 3584, 3840), ("s", 3840, 4096)),
)


def tile_moe_two_lin_gelu_kernel(tc, xT, w_words, w_scales, b, gate, offs, dst, out):
    nc = tc.nc
    gelu = mybir.ActivationFunctionType.Gelu_apprx_tanh
    mult = mybir.AluOpType.mult

    with tc.tile_pool(name="keep", bufs=1) as keep, tc.psum_pool(name="psum", bufs=1) as psum:
        offs_t = keep.tile([P, SLOTS // 16], U16, name="offs_t")
        dst_t = keep.tile([P, SLOTS // 16], U16, name="dst_t")
        raw_0 = keep.tile([P, 2, T], F32, name="raw_0")
        raw_1 = [keep.tile([P, 2, c1 - c0], F32, name=f"raw_1_{c0}") for c0, c1 in CHUNKS[1]]
        words = [keep.tile([P, 2 * T], BF16, name=f"words{u}", align_bytes=64) for u in range(2)]
        grouped_ab = keep.tile([P, 8 * G], BF16, name="grouped_ab", align_bytes=64)
        grouped_cd = keep.tile([P, 8 * G], BF16, name="grouped_cd", align_bytes=64)
        codes = keep.tile([P, SLOTS], U32, name="codes", align_bytes=64)
        late_cd = keep.tile([P, 4 * G], BF16, name="late_cd", align_bytes=64)
        scales = keep.tile([P, SLOTS], U8, name="scales", align_bytes=64)
        w_t = keep.tile([P, E, 2 * N], U8, name="w_t", align_bytes=64)
        ws_t = keep.tile([P, E, N], U8, name="ws_t", align_bytes=64)
        b_t = keep.tile([P, E], F32, name="b_t")
        gate_t = [keep.tile([P, n], F32, name=f"gate{i}") for i, n in enumerate((G, 3 * G))]
        y_a = keep.tile([P, G], F32, name="y_a")
        y_bcd = keep.tile([P, 3 * G], F32, name="y_bcd")
        out_t = keep.tile([P, T], F32, name="out_t")
        warm = keep.tile([P, 1], F32, name="warm")
        acc = [psum.tile([P, G], F32, name=f"acc{g}") for g in range(4)]

        x_rows = xT.rearrange("(p t) w -> p t w", t=4)
        ws_rows = w_scales.bitcast(I32).rearrange("e a q n -> (a q) e n")
        w_rows = w_words.bitcast(I32).rearrange("e a p n -> p (e a) n")

        def load_weights(e0, e1):
            for q in range(4):
                nc.sync.dma_start(out=ws_t[32 * q : 32 * q + 4, e0:e1, :].bitcast(I32), in_=ws_rows[4 * q : 4 * q + 4, e0:e1])
            nc.sync.dma_start(out=w_t[:, e0:e1, :].bitcast(I32), in_=w_rows[:, e0:e1, :])

        nc.vector.memset(warm[:], 0.0)
        nc.scalar.activation(out=warm[:], in_=warm[:], func=gelu)
        nc.vector.memset(ws_t[:].rearrange("p e n -> p (e n)").bitcast(I32), 0)
        nc.gpsimd.memset(out_t[:], 0.0)

        nc.sync.dma_start(out=raw_0[:, 0, :], in_=x_rows[:, 0, :])
        nc.sync.dma_start(offs_t[:], offs)
        for c0, c1 in CHUNKS[0]:
            nc.sync.dma_start(out=raw_0[:, 1, c0:c1], in_=x_rows[:, 1, c0:c1])
        for i, (c0, c1) in enumerate(CHUNKS[1]):
            nc.sync.dma_start(out=raw_1[i][:], in_=x_rows[:, 2:4, c0:c1])
        load_weights(0, 4)
        nc.sync.dma_start(b_t[:], b)
        load_weights(4, E)
        nc.sync.dma_start(dst_t[:], dst)
        for i, (s0, s1) in enumerate(((0, G), (G, 4 * G))):
            nc.sync.dma_start(out=gate_t[i][:], in_=gate[:, s0:s1])

        def slots(grouped, s0, s1):
            return grouped[:, 4 * s0 : 4 * s1].rearrange("p (n t) -> p n t", t=4)

        def cast(u, engine, c0, c1):
            if u == 0:
                raw = raw_0[:, :, c0:c1]
            else:
                i = [c[0] <= c0 and c1 <= c[1] for c in CHUNKS[1]].index(True)
                base = CHUNKS[1][i][0]
                raw = raw_1[i][:, :, c0 - base : c1 - base]
            to = words[u][:, 2 * c0 : 2 * c1].rearrange("p (n t) -> p n t", t=2)
            src = raw.rearrange("p t n -> p n t")
            if engine == "v":
                nc.vector.tensor_copy(out=to, in_=src)
            else:
                nc.scalar.copy(out=to, in_=src)

        def gather(to, u, s0, s1):
            nc.vector.tensor_copy(to, words[u][:].bitcast(U32).indirect(offs_t[:, s0 // 16 : s1 // 16]))

        def stepped(grouped, u):
            return grouped[:].bitcast(U32).rearrange("p (n u) -> p u n", u=2)[:, u, :]

        def merge(grouped, late, s0, s1):
            nc.scalar.copy(out=slots(grouped, s0, s1)[:, :, 2:4], in_=late[:, 2 * s0 : 2 * s1].rearrange("p (n t) -> p n t", t=2))

        def quantize(grouped, s0, s1):
            nc.vector.quantize_mx(out=codes[:, s0:s1].bitcast(FP8X4), scales=scales[:, s0:s1], in_=grouped)

        def multiply(g, y, y_base):
            for pass_kind in ("matmul", "gelu"):
                for i in range(4):
                    e = 4 * g + i
                    a = acc[g][:, i * N : (i + 1) * N]
                    if pass_kind == "matmul":
                        nc.tensor.matmul_mx(
                            out=a,
                            lhsT=w_t[:, e, :].bitcast(FP4X4),
                            lhsT_scale=ws_t[:, e, :],
                            rhs=codes[:, e * N : (e + 1) * N].bitcast(FP8X4),
                            rhs_scale=scales[:, e * N : (e + 1) * N],
                            start=True,
                            stop=True,
                        )
                    else:
                        nc.scalar.activation(out=y[:, e * N - y_base : (e + 1) * N - y_base], in_=a, func=gelu, bias=b_t[:, e : e + 1])

        def scatter(i, y, s0, s1):
            nc.vector.tensor_tensor(out_t[:].indirect(dst_t[:, s0 // 16 : s1 // 16]), y[:], gate_t[i][:], mult)

        for c in CASTS[0]:
            cast(0, *c)
        gather(stepped(grouped_ab, 0), 0, 0, 2 * G)
        gather(stepped(grouped_cd, 0), 0, 2 * G, 4 * G)
        for c in CASTS[1]:
            cast(1, *c)
        gather(late_cd[:].bitcast(U32), 1, 2 * G, 4 * G)
        merge(grouped_cd, late_cd, 0, G)
        merge(grouped_cd, late_cd, G, 2 * G)
        gather(stepped(grouped_ab, 1)[:, 0:G], 1, 0, G)
        gather(stepped(grouped_ab, 1)[:, G : 2 * G], 1, G, 2 * G)
        quantize(grouped_ab[:, 0 : 4 * G], 0, G)
        multiply(A, y_a, 0)
        quantize(grouped_ab[:, 4 * G : 8 * G], G, 2 * G)
        multiply(B, y_bcd, G)
        quantize(grouped_cd[:], 2 * G, 4 * G)
        multiply(C, y_bcd, G)
        multiply(D, y_bcd, G)
        scatter(0, y_a, 0, G)
        scatter(1, y_bcd, G, 4 * G)
        nc.sync.dma_start(out, out_t[:])
